import numpy as np, ml_dtypes
CORES = [9,25,41,57]
N = 4
import mx_ref
BF = ml_dtypes.bfloat16
def entries(a):
    return np.ascontiguousarray(a.T).reshape(-1)
def table(e):
    return np.ascontiguousarray(np.reshape(e, (-1, 16)).T).astype(np.int32)
def gentries(a):
    return np.ascontiguousarray(a.reshape(8, 16, -1).transpose(0, 2, 1)).reshape(8, -1)
def gtable(e):
    e = np.asarray(e); return np.ascontiguousarray(e.reshape(8, -1, 16).transpose(0, 2, 1)).reshape(128, -1).astype(np.int32)
def cols(t, e):
    v = np.concatenate([t.reshape(128, -1, 4), np.zeros((128, 1, 4), BF)], axis=1)
    return np.ascontiguousarray(v[:, e]).reshape(128, -1)
def gpick(z, e):
    return np.concatenate([z[16 * g:16 * g + 16][:, e[g]] for g in range(8)])
def tile(rs):
    return np.stack(rs, axis=2).reshape(128, -1).astype(BF)
def cut(t, i, w=512):
    return t[:, w * i:w * i + w]
def f(rng, *shape):
    return mx_ref.flush((rng.standard_normal(shape, dtype=np.float32) * np.exp2(rng.integers(-2, 3, shape[:-1] + (1,)))).astype(BF))
def wide(rng, *shape, cols=0):
    v = rng.standard_normal(shape, dtype=np.float32) * np.exp2(rng.integers(-12, 13, shape)).astype(np.float32)
    if cols: v *= np.repeat(np.exp2(rng.integers(-cols, cols + 1, shape[:-2] + (1, shape[-1] // 4))) * (rng.random(shape[:-2] + (1, shape[-1] // 4)) > 0.0625), 4, axis=-1).astype(np.float32)
    return mx_ref.flush(v.astype(BF))
T, CAPP, KH, O = 512, 128, 512, 2
def lists(rng, kind="plain"):
    g = np.full((N, N * CAPP), -1)
    for s in range(N):
        for d in range(N):
            if d == s: continue
            n = rng.integers(0, CAPP + 1)
            if kind in ("foreign", "one"): n = CAPP
            if kind == "own": n = CAPP if d == (s + 1) % N else 0
            g[s, d * CAPP + rng.permutation(CAPP)[:n]] = rng.permutation(T)[:n] if n == CAPP else rng.integers(0, T, n)
    p = []
    for r in range(N):
        near = np.arange(T)
        far = T + np.flatnonzero(g[:, r * CAPP:(r + 1) * CAPP].reshape(-1) >= 0)
        if len(far) == 0: far = near
        e = np.where(rng.random((8, KH)) < 0.5, rng.choice(near, (8, KH)), rng.choice(far, (8, KH)))
        if kind == "agree": e = np.repeat(e[:1], 8, axis=0)
        if kind == "foreign": e = rng.choice(far, (8, KH))
        if kind == "own": e = rng.choice(near, (8, KH))
        if kind == "one":
            k = rng.permutation(np.concatenate([rng.permutation(near)[:4], rng.permutation(far)[:4]]))
            e = np.repeat(k[:, None], KH, axis=1)
        p.append(gtable(e))
    return {"snd": np.stack([table(g[s]) for s in range(N)]), "pk": np.stack(p)}
def setup_inputs(rng):
    return {"x": f(rng, N, 128, 4 * T), "w": f(rng, N, 128, 2048), "v": f(rng, N, 128, O * 512), **lists(rng)}
def setup_inputs_agree(rng):
    return {**setup_inputs(rng), **lists(rng, "agree")}
def setup_inputs_foreign(rng):
    return {**setup_inputs(rng), **lists(rng, "foreign")}
def setup_inputs_own(rng):
    return {**setup_inputs(rng), **lists(rng, "own")}
def setup_inputs_one(rng):
    return {**setup_inputs(rng), **lists(rng, "one")}
def setup_inputs_spread(rng):
    d = setup_inputs(rng); d["x"] = wide(rng, N, 128, 4 * T, cols=8); return d
def check_inputs(d):
    b = []
    g = np.stack([entries(d["snd"][s]) for s in range(N)])
    for r in range(N):
        if g[r].min() < -1 or g[r].max() >= T or (g[r, r * CAPP:(r + 1) * CAPP] != -1).any(): b.append("snd")
        e = gentries(d["pk"][r])
        if e.min() < 0 or e.max() >= T + N * CAPP: b.append("pk")
        else:
            used = g[:, r * CAPP:(r + 1) * CAPP].reshape(-1) >= 0
            if not used[e[e >= T] - T].all(): b.append("pk")
    return b
def reference(x, w, v, snd, pk):
    y = np.zeros((N, 128, O * KH), np.float32)
    for r in range(N):
        t = np.concatenate([x[r]] + [cols(x[s], entries(snd[s])[r * CAPP:(r + 1) * CAPP]) for s in range(N)], axis=1)
        q = mx_ref.quantize(np.ascontiguousarray(t))
        e = gentries(pk[r])
        rs = []
        for b in range(4):
            z = mx_ref.matmul(mx_ref.quantize(np.ascontiguousarray(cut(w[r], b))), q)
            rs.append(np.maximum(gpick(z, e), np.float32(0)) * np.float32(0.05))
        h = mx_ref.quantize(np.ascontiguousarray(tile(rs)))
        for o in range(O): y[r][:, KH * o:KH * o + KH] = mx_ref.matmul(mx_ref.quantize(np.ascontiguousarray(cut(v[r], o))), h)
    return {"y": y}

@@ -1,0 +1,210 @@
+from concourse.mybir import dt, AluOpType, ActivationFunctionType
+
+RELU = ActivationFunctionType.Relu
+COPY = ActivationFunctionType.Copy
+
+SCRATCH = {
+    "sn": ("sbuf", [128, 32], "int32"),
+    "pi": ("sbuf", [128, 32], "int32"),
+    "po": ("sbuf", [128, 32], "uint16"),
+    "xt": ("sbuf", [128, 2048], "bfloat16"),
+    "wt": ("sbuf", [128, 2048], "bfloat16"),
+    "vt": ("sbuf", [128, 1024], "bfloat16"),
+    "xq": ("sbuf", [128, 512], "float8_e4m3fn_x4"),
+    "xp": ("sbuf", [128, 512], "uint8"),
+    "wq": ("sbuf", [128, 512], "float8_e4m3fn_x4"),
+    "wp": ("sbuf", [128, 512], "uint8"),
+    "vq": ("sbuf", [128, 256], "float8_e4m3fn_x4"),
+    "vp": ("sbuf", [128, 256], "uint8"),
+    "ht": ("sbuf", [128, 2048], "bfloat16"),
+    "hq": ("sbuf", [128, 512], "float8_e4m3fn_x4"),
+    "hp": ("sbuf", [128, 512], "uint8"),
+    "ys": ("sbuf", [128, 1024], "float32"),
+    "pa": ("psum", [128, 2048], "float32"),
+    "pb": ("psum", [128, 2048], "float32"),
+}
+for _t in range(4):
+    SCRATCH["of%d" % _t] = ("sbuf", [128, 32], "uint16")
+    SCRATCH["z%d" % _t] = ("sbuf", [128, 1024], "float32")
+for _j in range(3):
+    SCRATCH["st%d" % _j] = ("sbuf", [128, 512], "bfloat16")
+    SCRATCH["sq%d" % _j] = ("sbuf", [128, 128], "float8_e4m3fn_x4")
+    SCRATCH["sp%d" % _j] = ("sbuf", [128, 128], "uint8")
+    SCRATCH["lq%d" % _j] = ("sbuf", [128, 128], "float8_e4m3fn_x4")
+    SCRATCH["lp%d" % _j] = ("sbuf", [128, 128], "uint8")
+
+SEMAPHORES = ["sn", "xa", "xb", "w", "v", "pk", "mz", "off", "po", "qin", "qv", "sent", "yd", "ye"]
+SEMAPHORES += ["g%d" % j for j in range(3)] + ["q%d" % j for j in range(3)] + ["arr%d" % j for j in range(3)]
+SEMAPHORES += ["om%d" % b for b in range(4)] + ["oc%d" % b for b in range(4)]
+SEMAPHORES += ["fm%d%d" % (j, b) for j in range(3) for b in range(4)] + ["fc%d%d" % (j, b) for j in range(3) for b in range(4)]
+SEMAPHORES += ["hg%d" % c for c in range(2)] + ["hq%d" % c for c in range(2)]
+SEMAPHORES += ["ym%d%d" % (c, o) for c in range(2) for o in range(2)] + ["yc%d%d" % (c, o) for c in range(2) for o in range(2)]
+
+V_B, S_B = (0, 1), (2, 3)
+ORDER = (0, 2, 1, 3)
+HALVES = ((0, 256), (256, 512))
+
+
+def rank_program(g, core, T, topo):
+    rank = T.rank_of(core)
+    if rank is None:
+        return
+    n_ranks = len(T.cores)
+    t_cols, cap, kh = 512, 128, 512
+    dests = [(rank + 1 + j) % n_ranks for j in range(n_ranks - 1)]
+    froms = [(rank - 1 - j) % n_ranks for j in range(n_ranks - 1)]
+    S = T.sem
+    vec, sca, ten, syn = g.vector, g.scalar, g.tensor, g.sync
+
+    syn.dma_start(T.xt[:, 0:1024], T.x[:, 0:1024]).then_inc(S.xa, 16)
+    for i in range(4):
+        sca.dma_start(T.sn[16 * i:16 * i + 16, :], T.snd[:, :]).then_inc(S.sn, 16)
+    sca.dma_start(T.xt[:, 1024:2048], T.x[:, 1024:2048]).then_inc(S.xb, 16)
+    sca.dma_start(T.wt[:, :], T.w[:, :]).then_inc(S.w, 16)
+    sca.dma_start(T.pi[:, :], T.pk[:, :]).then_inc(S.pk, 16)
+    syn.wait_ge(S.q1, 1)
+    syn.dma_start(T.vt[:, :], T.v[:, :]).then_inc(S.v, 16)
+
+    for b in range(4):
+        a = t_cols + cap * rank
+        vec.memset(T["z%d" % b][:, a:a + cap], 0.0).then_inc(S.mz, 1)
+    vec.wait_ge(S.sn, 64)
+    for t in range(4):
+        for lo in (0, 64):
+            vec.tensor_scalar(T["of%d" % t][lo:lo + 64, :], T.sn[0:64, :], 4.0, float(t), AluOpType.mult, AluOpType.add).then_inc(S.off, 1)
+    vec.wait_ge(S.xa, 16)
+    vec.quantize_mx(T.xq[:, 0:256], T.xp[:, 0:256], T.xt[:, 0:1024]).then_inc(S.qin, 1)
+
+    for q in (vec, sca):
+        q.wait_ge(S.off, 8)
+        q.wait_ge(S.xa, 16)
+        q.wait_ge(S.xb, 16)
+    for j, d in enumerate(dests):
+        a = d * cap // 16
+        tile = T["st%d" % j]
+        for t in V_B:
+            vec.tensor_copy(tile[:, t:512:4], T.xt[:, 0:2048].indirect(T["of%d" % t][:, a:a + 8])).then_inc(S["g%d" % j], 1)
+        for t in S_B:
+            sca.activation(tile[:, t:512:4], T.xt[:, 0:2048].indirect(T["of%d" % t][:, a:a + 8]), COPY).then_inc(S["g%d" % j], 1)
+        vec.wait_ge(S["g%d" % j], 4)
+        vec.quantize_mx(T["sq%d" % j][:, :], T["sp%d" % j][:, :], tile[:, :]).then_inc(S["q%d" % j], 1)
+        dst = T.cores[d]
+        rid, pid, _ = topo.addr(dst)
+        m = topo.mask(core, dst)
+        g.wait_ge(S["q%d" % j], 1)
+        g.remote_dma(T["lq%d" % j][:, :].bitcast(dt.uint8), T["sq%d" % j][:, :].bitcast(dt.uint8), S["arr%d" % j], S.sent, pid, rid, m)
+        g.remote_dma(T["lp%d" % j][:, :], T["sp%d" % j][:, :], S["arr%d" % j], S.sent, pid, rid, m)
+    incs = [2 * len(topo.engines(core, T.cores[d])) for d in dests]
+    arr = [2 * len(topo.engines(T.cores[s], core)) for s in froms]
+    g.wait_ge(S.sent, sum(incs))
+
+    vec.quantize_mx(T.xq[:, 256:512], T.xp[:, 256:512], T.xt[:, 1024:2048]).then_inc(S.qin, 1)
+    vec.wait_ge(S.w, 16)
+    vec.quantize_mx(T.wq[:, :], T.wp[:, :], T.wt[:, :]).then_inc(S.qin, 1)
+    vec.wait_ge(S.pk, 16)
+    vec.tensor_copy(T.po[:, :], T.pi[:, :]).then_inc(S.po, 1)
+
+    ten.wait_ge(S.qin, 3)
+    for b in ORDER:
+        ten.matmul_mx(T.pa[:, 512 * b:512 * b + 512], T.wq[:, 128 * b:128 * b + 128], T.wp[:, 128 * b:128 * b + 128],
+                      T.xq[:, :], T.xp[:, :], True, True).then_inc(S["om%d" % b], 1)
+    for b in V_B:
+        vec.wait_ge(S["om%d" % b], 1)
+        vec.tensor_copy(T["z%d" % b][:, 0:512], T.pa[:, 512 * b:512 * b + 512]).then_inc(S["oc%d" % b], 1)
+    for b in S_B:
+        sca.wait_ge(S["om%d" % b], 1)
+        sca.activation(T["z%d" % b][:, 0:512], T.pa[:, 512 * b:512 * b + 512], COPY).then_inc(S["oc%d" % b], 1)
+    vec.wait_ge(S.v, 16)
+    vec.quantize_mx(T.vq[:, :], T.vp[:, :], T.vt[:, :]).then_inc(S.qv, 1)
+
+    for j, s in enumerate(froms):
+        ps = T.pb if j % 2 == 0 else T.pa
+        ten.wait_ge(S["arr%d" % j], arr[j])
+        for b in ORDER:
+            if j == 1:
+                ten.wait_ge(S["oc%d" % b], 1)
+            if j == 2:
+                ten.wait_ge(S["fc0%d" % b], 1)
+            ten.matmul_mx(ps[:, 512 * b:512 * b + cap], T.wq[:, 128 * b:128 * b + 128], T.wp[:, 128 * b:128 * b + 128],
+                          T["lq%d" % j][:, :], T["lp%d" % j][:, :], True, True).then_inc(S["fm%d%d" % (j, b)], 1)
+        a = t_cols + cap * s
+        for b in V_B:
+            vec.wait_ge(S["fm%d%d" % (j, b)], 1)
+            vec.tensor_copy(T["z%d" % b][:, a:a + cap], ps[:, 512 * b:512 * b + cap]).then_inc(S["fc%d%d" % (j, b)], 1)
+        for b in S_B:
+            sca.wait_ge(S["fm%d%d" % (j, b)], 1)
+            sca.activation(T["z%d" % b][:, a:a + cap], ps[:, 512 * b:512 * b + cap], COPY).then_inc(S["fc%d%d" % (j, b)], 1)
+
+    def ready(q, b):
+        q.wait_ge(S["oc%d" % b], 1)
+        for j in range(3):
+            q.wait_ge(S["fc%d%d" % (j, b)], 1)
+
+    def pick(c, b):
+        lo, hi = HALVES[c]
+        src = T["z%d" % b][:, 0:1024].indirect(T.po[:, lo // 16:hi // 16])
+        out = T.ht[:, 4 * lo + b:4 * hi:4]
+        if b in V_B:
+            vec.tensor_scalar(out, src, 0.0, 0.05, AluOpType.max, AluOpType.mult).then_inc(S["hg%d" % c], 1)
+        else:
+            sca.activation(out, src, RELU, scale=0.05).then_inc(S["hg%d" % c], 1)
+
+    def quant(c):
+        lo, hi = HALVES[c]
+        vec.wait_ge(S["hg%d" % c], 4)
+        vec.quantize_mx(T.hq[:, lo:hi], T.hp[:, lo:hi], T.ht[:, 4 * lo:4 * hi]).then_inc(S["hq%d" % c], 1)
+
+    def bank(c, o):
+        lo, hi = HALVES[c]
+        return T.pa[:, 512 * (2 * c + o):512 * (2 * c + o) + hi - lo]
+
+    def out_of_psum(c, o):
+        lo, hi = HALVES[c]
+        out = T.ys[:, kh * o + lo:kh * o + hi]
+        if o == 0:
+            vec.wait_ge(S["ym%d%d" % (c, o)], 1)
+            vec.tensor_copy(out, bank(c, o)).then_inc(S["yc%d%d" % (c, o)], 1)
+        else:
+            sca.wait_ge(S["ym%d%d" % (c, o)], 1)
+            sca.activation(out, bank(c, o), COPY).then_inc(S["yc%d%d" % (c, o)], 1)
+
+    def store(q, sem, c, o):
+        lo, hi = HALVES[c]
+        q.wait_ge(S["yc%d%d" % (c, o)], 1)
+        q.dma_start(T.y[:, kh * o + lo:kh * o + hi], T.ys[:, kh * o + lo:kh * o + hi]).then_inc(sem, 16)
+
+    for q in (vec, sca):
+        q.wait_ge(S.mz, 4)
+        q.wait_ge(S.po, 1)
+    ten.wait_ge(S.qv, 1)
+    for c in range(2):
+        ten.wait_ge(S["hq%d" % c], 1)
+        lo, hi = HALVES[c]
+        for o in range(2):
+            ten.wait_ge(S["fc1%d" % (2 * c + o)], 1)
+            ten.matmul_mx(bank(c, o), T.vq[:, 128 * o:128 * o + 128], T.vp[:, 128 * o:128 * o + 128],
+                          T.hq[:, lo:hi], T.hp[:, lo:hi], True, True).then_inc(S["ym%d%d" % (c, o)], 1)
+    ready(vec, 0)
+    pick(0, 0)
+    ready(vec, 1)
+    pick(0, 1)
+    quant(0)
+    pick(1, 0)
+    out_of_psum(0, 0)
+    pick(1, 1)
+    quant(1)
+    out_of_psum(1, 0)
+    ready(sca, 2)
+    pick(0, 2)
+    ready(sca, 3)
+    pick(0, 3)
+    pick(1, 2)
+    pick(1, 3)
+    out_of_psum(0, 1)
+    out_of_psum(1, 1)
+    store(syn, S.yd, 0, 0)
+    store(syn, S.yd, 0, 1)
+    store(syn, S.yd, 1, 0)
+    store(sca, S.ye, 1, 1)
+    syn.wait_ge(S.yd, 48)
+    sca.wait_ge(S.ye, 16)

@@ -3,6 +3,8 @@ from concourse.mybir import dt, AluOpType, ActivationFunctionType
 RELU = ActivationFunctionType.Relu
 COPY = ActivationFunctionType.Copy
 
+CHUNKS = ((0, 192), (192, 384), (384, 512))
+
 SCRATCH = {
     "sn": ("sbuf", [128, 32], "int32"),
     "pi": ("sbuf", [128, 32], "int32"),
@@ -33,16 +35,21 @@ for _j in range(3):
     SCRATCH["lq%d" % _j] = ("sbuf", [128, 128], "float8_e4m3fn_x4")
     SCRATCH["lp%d" % _j] = ("sbuf", [128, 128], "uint8")
 
-SEMAPHORES = ["sn", "xa", "xb", "w", "v", "pk", "mz", "off", "po", "qin", "qv", "sent", "yd", "ye"]
-SEMAPHORES += ["g%d" % j for j in range(3)] + ["q%d" % j for j in range(3)] + ["arr%d" % j for j in range(3)]
-SEMAPHORES += ["om%d" % b for b in range(4)] + ["oc%d" % b for b in range(4)]
-SEMAPHORES += ["fm%d%d" % (j, b) for j in range(3) for b in range(4)] + ["fc%d%d" % (j, b) for j in range(3) for b in range(4)]
-SEMAPHORES += ["hg%d" % c for c in range(2)] + ["hq%d" % c for c in range(2)]
-SEMAPHORES += ["ym%d%d" % (c, o) for c in range(2) for o in range(2)] + ["yc%d%d" % (c, o) for c in range(2) for o in range(2)]
+PLAN = {
+    "vec": "zero of0 of1 g00 g01 q0 g10 qx q1 g20 qw0 q2 qw1 qw2 qw3 po qv oc1 oc3 fc03 fc11 fc13 fc21 fc23 "
+           "p01 p03 p11 qh0 p13 qh1 p21 p23 qh2 yc21",
+    "sca": "sn1 g02 g03 g11 g12 g13 g21 g22 g23 oc0 oc2 fc00 fc01 fc02 fc10 fc12 fc20 fc22 "
+           "p00 p02 p10 p12 p20 yc00 yc01 p22 yc10 yc11 yc20 st20",
+    "ten": "om0 om1 om2 om3 fm00 fm01 fm02 fm03 fm10 fm11 fm12 fm13 fm20 fm21 fm22 fm23 ym00 ym01 ym10 ym11 ym20 ym21",
+    "syn": "sn0 x w0 w1 v pk st00 st01 st10 st11 st21",
+    "g": "send0 send1 send2",
+}
 
-V_B, S_B = (0, 1), (2, 3)
-ORDER = (0, 2, 1, 3)
-HALVES = ((0, 256), (256, 512))
+SEMAPHORES = ["sn", "x", "w0", "w1", "v", "pk", "zero", "of0", "of1", "po", "qx", "qv", "sent", "yd", "ye"]
+SEMAPHORES += [s % j for j in range(3) for s in ("g%d", "q%d", "arr%d", "p%d", "qh%d")]
+SEMAPHORES += [s % b for b in range(4) for s in ("qw%d", "om%d", "oc%d")]
+SEMAPHORES += [s % (j, b) for j in range(3) for b in range(4) for s in ("fm%d%d", "fc%d%d")]
+SEMAPHORES += [s % (c, o) for c in range(3) for o in range(2) for s in ("ym%d%d", "yc%d%d")]
 
 
 def rank_program(g, core, T, topo):
@@ -54,157 +61,144 @@ def rank_program(g, core, T, topo):
     dests = [(rank + 1 + j) % n_ranks for j in range(n_ranks - 1)]
     froms = [(rank - 1 - j) % n_ranks for j in range(n_ranks - 1)]
     S = T.sem
-    vec, sca, ten, syn = g.vector, g.scalar, g.tensor, g.sync
+    queues = {"vec": g.vector, "sca": g.scalar, "ten": g.tensor, "syn": g.sync, "g": g}
+    full = {"sn": 32, "x": 16, "w0": 16, "w1": 16, "v": 16, "pk": 16, "zero": 4, "of0": 4, "of1": 3}
+    for j in range(3):
+        full["g%d" % j] = full["p%d" % j] = 4
+        full["arr%d" % j] = 2 * len(topo.engines(T.cores[froms[j]], core))
+    stores = {"syn": [0, S.yd], "sca": [0, S.ye]}
 
-    syn.dma_start(T.xt[:, 0:1024], T.x[:, 0:1024]).then_inc(S.xa, 16)
-    for i in range(4):
-        sca.dma_start(T.sn[16 * i:16 * i + 16, :], T.snd[:, :]).then_inc(S.sn, 16)
-    sca.dma_start(T.xt[:, 1024:2048], T.x[:, 1024:2048]).then_inc(S.xb, 16)
-    sca.dma_start(T.wt[:, :], T.w[:, :]).then_inc(S.w, 16)
-    sca.dma_start(T.pi[:, :], T.pk[:, :]).then_inc(S.pk, 16)
-    syn.wait_ge(S.q1, 1)
-    syn.dma_start(T.vt[:, :], T.v[:, :]).then_inc(S.v, 16)
+    def move(name, out, src):
+        if name == "vec":
+            return g.vector.tensor_copy(out, src)
+        return g.scalar.activation(out, src, COPY)
 
-    for b in range(4):
-        a = t_cols + cap * rank
-        vec.memset(T["z%d" % b][:, a:a + cap], 0.0).then_inc(S.mz, 1)
-    vec.wait_ge(S.sn, 64)
-    for t in range(4):
-        for lo in (0, 64):
-            vec.tensor_scalar(T["of%d" % t][lo:lo + 64, :], T.sn[0:64, :], 4.0, float(t), AluOpType.mult, AluOpType.add).then_inc(S.off, 1)
-    vec.wait_ge(S.xa, 16)
-    vec.quantize_mx(T.xq[:, 0:256], T.xp[:, 0:256], T.xt[:, 0:1024]).then_inc(S.qin, 1)
+    def product(out, sq, sp, i, mq, mp):
+        return g.tensor.matmul_mx(out, sq[:, 128 * i:128 * i + 128], sp[:, 128 * i:128 * i + 128], mq, mp, True, True)
 
-    for q in (vec, sca):
-        q.wait_ge(S.off, 8)
-        q.wait_ge(S.xa, 16)
-        q.wait_ge(S.xb, 16)
-    for j, d in enumerate(dests):
-        a = d * cap // 16
-        tile = T["st%d" % j]
-        for t in V_B:
-            vec.tensor_copy(tile[:, t:512:4], T.xt[:, 0:2048].indirect(T["of%d" % t][:, a:a + 8])).then_inc(S["g%d" % j], 1)
-        for t in S_B:
-            sca.activation(tile[:, t:512:4], T.xt[:, 0:2048].indirect(T["of%d" % t][:, a:a + 8]), COPY).then_inc(S["g%d" % j], 1)
-        vec.wait_ge(S["g%d" % j], 4)
-        vec.quantize_mx(T["sq%d" % j][:, :], T["sp%d" % j][:, :], tile[:, :]).then_inc(S["q%d" % j], 1)
-        dst = T.cores[d]
-        rid, pid, _ = topo.addr(dst)
-        m = topo.mask(core, dst)
-        g.wait_ge(S["q%d" % j], 1)
-        g.remote_dma(T["lq%d" % j][:, :].bitcast(dt.uint8), T["sq%d" % j][:, :].bitcast(dt.uint8), S["arr%d" % j], S.sent, pid, rid, m)
-        g.remote_dma(T["lp%d" % j][:, :], T["sp%d" % j][:, :], S["arr%d" % j], S.sent, pid, rid, m)
-    incs = [2 * len(topo.engines(core, T.cores[d])) for d in dests]
-    arr = [2 * len(topo.engines(T.cores[s], core)) for s in froms]
-    g.wait_ge(S.sent, sum(incs))
+    def arrival_bank(j, b):
+        return (T.pa if j % 2 else T.pb)[:, 512 * b:512 * b + cap]
 
-    vec.quantize_mx(T.xq[:, 256:512], T.xp[:, 256:512], T.xt[:, 1024:2048]).then_inc(S.qin, 1)
-    vec.wait_ge(S.w, 16)
-    vec.quantize_mx(T.wq[:, :], T.wp[:, :], T.wt[:, :]).then_inc(S.qin, 1)
-    vec.wait_ge(S.pk, 16)
-    vec.tensor_copy(T.po[:, :], T.pi[:, :]).then_inc(S.po, 1)
+    def y_bank(c, o):
+        lo, hi = CHUNKS[c]
+        i = 2 * c + o
+        return (T.pa if i < 4 else T.pb)[:, 512 * (i % 4):512 * (i % 4) + hi - lo], "fc%d%d" % (1 if i < 4 else 2, i % 4)
 
-    ten.wait_ge(S.qin, 3)
-    for b in ORDER:
-        ten.matmul_mx(T.pa[:, 512 * b:512 * b + 512], T.wq[:, 128 * b:128 * b + 128], T.wp[:, 128 * b:128 * b + 128],
-                      T.xq[:, :], T.xp[:, :], True, True).then_inc(S["om%d" % b], 1)
-    for b in V_B:
-        vec.wait_ge(S["om%d" % b], 1)
-        vec.tensor_copy(T["z%d" % b][:, 0:512], T.pa[:, 512 * b:512 * b + 512]).then_inc(S["oc%d" % b], 1)
-    for b in S_B:
-        sca.wait_ge(S["om%d" % b], 1)
-        sca.activation(T["z%d" % b][:, 0:512], T.pa[:, 512 * b:512 * b + 512], COPY).then_inc(S["oc%d" % b], 1)
-    vec.wait_ge(S.v, 16)
-    vec.quantize_mx(T.vq[:, :], T.vp[:, :], T.vt[:, :]).then_inc(S.qv, 1)
+    def step(name, op, need):
+        q = queues[name]
+        kind, a = op.rstrip("0123456789"), [int(ch) for ch in op if ch.isdigit()]
+        if kind == "sn":
+            q.dma_start(T.sn[16 * a[0]:16 * a[0] + 16, :], T.snd[:, :]).then_inc(S.sn, 16)
+        elif op == "x":
+            q.dma_start(T.xt[:, :], T.x[:, :]).then_inc(S.x, 16)
+        elif kind == "w":
+            q.dma_start(T.wt[:, 1024 * a[0]:1024 * a[0] + 1024], T.w[:, 1024 * a[0]:1024 * a[0] + 1024]).then_inc(S[op], 16)
+        elif op == "v":
+            q.dma_start(T.vt[:, :], T.v[:, :]).then_inc(S.v, 16)
+        elif op == "pk":
+            q.dma_start(T.pi[:, :], T.pk[:, :]).then_inc(S.pk, 16)
+        elif op == "zero":
+            for b in range(4):
+                q.memset(T["z%d" % b][:, t_cols + cap * rank:t_cols + cap * rank + cap], 0.0).then_inc(S.zero, 1)
+        elif op == "of0":
+            need("sn")
+            for p in range(0, 128, 32):
+                q.tensor_scalar(T.of0[p:p + 32, :], T.sn[0:32, :], 4.0, None, AluOpType.mult).then_inc(S.of0, 1)
+        elif op == "of1":
+            need("of0")
+            for t in (2, 1, 3):
+                q.tensor_scalar(T["of%d" % t][:, :], T.of0[:, :], float(t), None, AluOpType.add).then_inc(S.of1, 1)
+        elif op == "po":
+            need("pk")
+            q.tensor_copy(T.po[:, :], T.pi[:, :]).then_inc(S.po, 1)
+        elif kind == "g":
+            j, t = a
+            need("of0", "of1", "x")
+            c = dests[j] * cap // 16
+            move(name, T["st%d" % j][:, t:512:4], T.xt[:, :].indirect(T["of%d" % t][:, c:c + 8])).then_inc(S["g%d" % j], 1)
+        elif kind == "q":
+            need("g%d" % a[0])
+            q.quantize_mx(T["sq%d" % a[0]][:, :], T["sp%d" % a[0]][:, :], T["st%d" % a[0]][:, :]).then_inc(S[op], 1)
+        elif kind == "send":
+            j = a[0]
+            dst = T.cores[dests[j]]
+            rid, pid, _ = topo.addr(dst)
+            m = topo.mask(core, dst)
+            need("q%d" % j)
+            q.remote_dma(T["lq%d" % j][:, :].bitcast(dt.uint8), T["sq%d" % j][:, :].bitcast(dt.uint8), S["arr%d" % j], S.sent, pid, rid, m)
+            q.remote_dma(T["lp%d" % j][:, :], T["sp%d" % j][:, :], S["arr%d" % j], S.sent, pid, rid, m)
+        elif op == "qx":
+            need("x")
+            q.quantize_mx(T.xq[:, :], T.xp[:, :], T.xt[:, :]).then_inc(S.qx, 1)
+        elif kind == "qw":
+            b = a[0]
+            need("w%d" % (b // 2))
+            q.quantize_mx(T.wq[:, 128 * b:128 * b + 128], T.wp[:, 128 * b:128 * b + 128], T.wt[:, 512 * b:512 * b + 512]).then_inc(S[op], 1)
+        elif op == "qv":
+            need("v")
+            q.quantize_mx(T.vq[:, :], T.vp[:, :], T.vt[:, :]).then_inc(S.qv, 1)
+        elif kind == "om":
+            b = a[0]
+            need("qx", "qw%d" % b)
+            product(T.pa[:, 512 * b:512 * b + 512], T.wq, T.wp, b, T.xq[:, :], T.xp[:, :]).then_inc(S[op], 1)
+        elif kind == "oc":
+            b = a[0]
+            need("om%d" % b)
+            move(name, T["z%d" % b][:, 0:t_cols], T.pa[:, 512 * b:512 * b + 512]).then_inc(S[op], 1)
+        elif kind == "fm":
+            j, b = a
+            need(*([], ["oc%d" % b], ["fc0%d" % b])[j])
+            need("qw%d" % b, "arr%d" % j)
+            product(arrival_bank(j, b), T.wq, T.wp, b, T["lq%d" % j][:, :], T["lp%d" % j][:, :]).then_inc(S[op], 1)
+        elif kind == "fc":
+            j, b = a
+            need("fm%d%d" % (j, b))
+            c = t_cols + cap * froms[j]
+            move(name, T["z%d" % b][:, c:c + cap], arrival_bank(j, b)).then_inc(S[op], 1)
+        elif kind == "p":
+            c, b = a
+            lo, hi = CHUNKS[c]
+            need("zero", "po", "oc%d" % b, "fc0%d" % b, "fc1%d" % b, "fc2%d" % b)
+            src = T["z%d" % b][:, :].indirect(T.po[:, lo // 16:hi // 16])
+            out = T.ht[:, 4 * lo + b:4 * hi:4]
+            if name == "vec":
+                q.tensor_scalar(out, src, 0.0, 0.05, AluOpType.max, AluOpType.mult).then_inc(S["p%d" % c], 1)
+            else:
+                q.activation(out, src, RELU, scale=0.05).then_inc(S["p%d" % c], 1)
+        elif kind == "qh":
+            lo, hi = CHUNKS[a[0]]
+            need("p%d" % a[0])
+            q.quantize_mx(T.hq[:, lo:hi], T.hp[:, lo:hi], T.ht[:, 4 * lo:4 * hi]).then_inc(S[op], 1)
+        elif kind == "ym":
+            c, o = a
+            lo, hi = CHUNKS[c]
+            bank, freed = y_bank(c, o)
+            need("qv", freed, "qh%d" % c)
+            product(bank, T.vq, T.vp, o, T.hq[:, lo:hi], T.hp[:, lo:hi]).then_inc(S[op], 1)
+        elif kind == "yc":
+            c, o = a
+            lo, hi = CHUNKS[c]
+            need("ym%d%d" % (c, o))
+            move(name, T.ys[:, kh * o + lo:kh * o + hi], y_bank(c, o)[0]).then_inc(S[op], 1)
+        elif kind == "st":
+            c, o = a
+            lo, hi = CHUNKS[c]
+            need("yc%d%d" % (c, o))
+            q.dma_start(T.y[:, kh * o + lo:kh * o + hi], T.ys[:, kh * o + lo:kh * o + hi]).then_inc(stores[name][1], 16)
+            stores[name][0] += 16
 
-    for j, s in enumerate(froms):
-        ps = T.pb if j % 2 == 0 else T.pa
-        ten.wait_ge(S["arr%d" % j], arr[j])
-        for b in ORDER:
-            if j == 1:
-                ten.wait_ge(S["oc%d" % b], 1)
-            if j == 2:
-                ten.wait_ge(S["fc0%d" % b], 1)
-            ten.matmul_mx(ps[:, 512 * b:512 * b + cap], T.wq[:, 128 * b:128 * b + 128], T.wp[:, 128 * b:128 * b + 128],
-                          T["lq%d" % j][:, :], T["lp%d" % j][:, :], True, True).then_inc(S["fm%d%d" % (j, b)], 1)
-        a = t_cols + cap * s
-        for b in V_B:
-            vec.wait_ge(S["fm%d%d" % (j, b)], 1)
-            vec.tensor_copy(T["z%d" % b][:, a:a + cap], ps[:, 512 * b:512 * b + cap]).then_inc(S["fc%d%d" % (j, b)], 1)
-        for b in S_B:
-            sca.wait_ge(S["fm%d%d" % (j, b)], 1)
-            sca.activation(T["z%d" % b][:, a:a + cap], ps[:, 512 * b:512 * b + cap], COPY).then_inc(S["fc%d%d" % (j, b)], 1)
+    for name in PLAN:
+        seen = []
 
-    def ready(q, b):
-        q.wait_ge(S["oc%d" % b], 1)
-        for j in range(3):
-            q.wait_ge(S["fc%d%d" % (j, b)], 1)
+        def need(*sems):
+            for s in sems:
+                if s not in seen:
+                    seen.append(s)
+                    queues[name].wait_ge(S[s], full.get(s, 1))
 
-    def pick(c, b):
-        lo, hi = HALVES[c]
-        src = T["z%d" % b][:, 0:1024].indirect(T.po[:, lo // 16:hi // 16])
-        out = T.ht[:, 4 * lo + b:4 * hi:4]
-        if b in V_B:
-            vec.tensor_scalar(out, src, 0.0, 0.05, AluOpType.max, AluOpType.mult).then_inc(S["hg%d" % c], 1)
-        else:
-            sca.activation(out, src, RELU, scale=0.05).then_inc(S["hg%d" % c], 1)
-
-    def quant(c):
-        lo, hi = HALVES[c]
-        vec.wait_ge(S["hg%d" % c], 4)
-        vec.quantize_mx(T.hq[:, lo:hi], T.hp[:, lo:hi], T.ht[:, 4 * lo:4 * hi]).then_inc(S["hq%d" % c], 1)
-
-    def bank(c, o):
-        lo, hi = HALVES[c]
-        return T.pa[:, 512 * (2 * c + o):512 * (2 * c + o) + hi - lo]
-
-    def out_of_psum(c, o):
-        lo, hi = HALVES[c]
-        out = T.ys[:, kh * o + lo:kh * o + hi]
-        if o == 0:
-            vec.wait_ge(S["ym%d%d" % (c, o)], 1)
-            vec.tensor_copy(out, bank(c, o)).then_inc(S["yc%d%d" % (c, o)], 1)
-        else:
-            sca.wait_ge(S["ym%d%d" % (c, o)], 1)
-            sca.activation(out, bank(c, o), COPY).then_inc(S["yc%d%d" % (c, o)], 1)
-
-    def store(q, sem, c, o):
-        lo, hi = HALVES[c]
-        q.wait_ge(S["yc%d%d" % (c, o)], 1)
-        q.dma_start(T.y[:, kh * o + lo:kh * o + hi], T.ys[:, kh * o + lo:kh * o + hi]).then_inc(sem, 16)
-
-    for q in (vec, sca):
-        q.wait_ge(S.mz, 4)
-        q.wait_ge(S.po, 1)
-    ten.wait_ge(S.qv, 1)
-    for c in range(2):
-        ten.wait_ge(S["hq%d" % c], 1)
-        lo, hi = HALVES[c]
-        for o in range(2):
-            ten.wait_ge(S["fc1%d" % (2 * c + o)], 1)
-            ten.matmul_mx(bank(c, o), T.vq[:, 128 * o:128 * o + 128], T.vp[:, 128 * o:128 * o + 128],
-                          T.hq[:, lo:hi], T.hp[:, lo:hi], True, True).then_inc(S["ym%d%d" % (c, o)], 1)
-    ready(vec, 0)
-    pick(0, 0)
-    ready(vec, 1)
-    pick(0, 1)
-    quant(0)
-    pick(1, 0)
-    out_of_psum(0, 0)
-    pick(1, 1)
-    quant(1)
-    out_of_psum(1, 0)
-    ready(sca, 2)
-    pick(0, 2)
-    ready(sca, 3)
-    pick(0, 3)
-    pick(1, 2)
-    pick(1, 3)
-    out_of_psum(0, 1)
-    out_of_psum(1, 1)
-    store(syn, S.yd, 0, 0)
-    store(syn, S.yd, 0, 1)
-    store(syn, S.yd, 1, 0)
-    store(sca, S.ye, 1, 1)
-    syn.wait_ge(S.yd, 48)
-    sca.wait_ge(S.ye, 16)
+        for op in PLAN[name].split():
+            step(name, op, need)
+    g.wait_ge(S.sent, sum(2 * len(topo.engines(core, T.cores[d])) for d in dests))
+    for name in stores:
+        if stores[name][0]:
+            queues[name].wait_ge(stores[name][1], stores[name][0])

@@ -1,9 +1,15 @@
+from concourse.bass import DstId, RemoteDMATransfer
 from concourse.mybir import dt, AluOpType, ActivationFunctionType
 
 RELU = ActivationFunctionType.Relu
 COPY = ActivationFunctionType.Copy
 
+PICKS = ((0, 192), (192, 384), (384, 512), (192, 512), (0, 384))
 CHUNKS = ((0, 192), (192, 384), (384, 512))
+STORES = ((0, 192), (512, 704), (192, 384), (704, 896), (384, 512), (896, 1024))
+TURN = 0
+W_PARTS = ((0, 4),)
+X_HEAD = 16
 
 SCRATCH = {
     "sn": ("sbuf", [128, 32], "int32"),
@@ -19,8 +25,8 @@ SCRATCH = {
     "vq": ("sbuf", [128, 256], "float8_e4m3fn_x4"),
     "vp": ("sbuf", [128, 256], "uint8"),
     "ht": ("sbuf", [128, 2048], "bfloat16"),
-    "hq": ("sbuf", [128, 512], "float8_e4m3fn_x4"),
-    "hp": ("sbuf", [128, 512], "uint8"),
+    "hq": ("sbuf", [128, 640], "float8_e4m3fn_x4"),
+    "hp": ("sbuf", [128, 640], "uint8"),
     "ys": ("sbuf", [128, 1024], "float32"),
     "pa": ("psum", [128, 2048], "float32"),
     "pb": ("psum", [128, 2048], "float32"),
@@ -36,20 +42,25 @@ for _j in range(3):
     SCRATCH["lp%d" % _j] = ("sbuf", [128, 128], "uint8")
 
 PLAN = {
-    "vec": "zero of0 of1 g00 g01 q0 g10 qx q1 g20 qw0 q2 qw1 qw2 qw3 po qv oc1 oc3 fc03 fc11 fc13 fc21 fc23 "
-           "p01 p03 p11 qh0 p13 qh1 p21 p23 qh2 yc21",
-    "sca": "sn1 g02 g03 g11 g12 g13 g21 g22 g23 oc0 oc2 fc00 fc01 fc02 fc10 fc12 fc20 fc22 "
-           "p00 p02 p10 p12 p20 yc00 yc01 p22 yc10 yc11 yc20 st20",
-    "ten": "om0 om1 om2 om3 fm00 fm01 fm02 fm03 fm10 fm11 fm12 fm13 fm20 fm21 fm22 fm23 ym00 ym01 ym10 ym11 ym20 ym21",
-    "syn": "sn0 x w0 w1 v pk st00 st01 st10 st11 st21",
-    "g": "send0 send1 send2",
+    "vec": "zero00 zero01 zero10 zero11 zero20 zero21 of2 zero30 of0 of3 of1 g00 g01 zero31 q0 qx0 qw0 qx1 q1 qw1 g23 qw2 q2 qw3 po qv oc01 oc03 oc13 "
+           "fc01 fc03 fc11 fc13 fc21 fc23 p41 p03 p13 qh0 p21 qh1 yc01 qh2 yc11 yc21",
+    "sca": "x0 x1 g02 g03 g10 g11 g12 g13 g20 g21 g22 oc00 oc10 oc11 oc02 oc12 "
+           "fc00 fc02 fc10 fc12 fc20 fc22 p40 p02 p32 p20 p23 yc00 yc10 yc20 st4",
+    "ten": "om00 om10 om01 om11 om02 om12 om03 om13 fm00 fm01 fm02 fm03 fm10 fm11 fm12 fm13 fm20 fm21 fm22 fm23 "
+           "ym01 ym00 ym11 ym10 ym20 ym21",
+    "syn": "sn0 sn1 w0 v pk st1 st0 st3 st2 st5",
+    "g": "sc0 sp0 sc1 sp1 sc2 sp2",
 }
+EVEN, ODD, ALL = slice(0, None, 2), slice(1, None, 2), slice(None)
+LANES = {"sc0": EVEN, "sp0": ODD, "sc1": ODD, "sp1": EVEN, "sc2": EVEN, "sp2": ODD}
 
-SEMAPHORES = ["sn", "x", "w0", "w1", "v", "pk", "zero", "of0", "of1", "po", "qx", "qv", "sent", "yd", "ye"]
-SEMAPHORES += [s % j for j in range(3) for s in ("g%d", "q%d", "arr%d", "p%d", "qh%d")]
-SEMAPHORES += [s % b for b in range(4) for s in ("qw%d", "om%d", "oc%d")]
-SEMAPHORES += [s % (j, b) for j in range(3) for b in range(4) for s in ("fm%d%d", "fc%d%d")]
-SEMAPHORES += [s % (c, o) for c in range(3) for o in range(2) for s in ("ym%d%d", "yc%d%d")]
+SEMAPHORES = ["sn", "x", "w0", "w1", "v", "pk", "of0", "of1", "of2", "of3", "po", "qx0", "qx1", "qv", "sent", "yd", "ye"]
+SEMAPHORES += [s % j for j in range(3) for s in ("g%d", "q%d", "arr%d")]
+SEMAPHORES += ["p%d" % c for c in range(len(PICKS))] + ["qh%d" % c for c in range(len(CHUNKS))]
+SEMAPHORES += [s % b for b in range(4) for s in ("qw%d", "z%d", "fc0%d")]
+SEMAPHORES += [s % (h, b) for h in range(2) for b in range(4) for s in ("om%d%d", "oc%d%d")]
+SEMAPHORES += ["fm%d%d" % (j, b) for j in range(3) for b in range(4)]
+SEMAPHORES += [s % (c, o) for c in range(len(CHUNKS)) for o in range(2) for s in ("ym%d%d", "yc%d%d")]
 
 
 def rank_program(g, core, T, topo):
@@ -62,10 +73,17 @@ def rank_program(g, core, T, topo):
     froms = [(rank - 1 - j) % n_ranks for j in range(n_ranks - 1)]
     S = T.sem
     queues = {"vec": g.vector, "sca": g.scalar, "ten": g.tensor, "syn": g.sync, "g": g}
-    full = {"sn": 32, "x": 16, "w0": 16, "w1": 16, "v": 16, "pk": 16, "zero": 4, "of0": 4, "of1": 3}
+    full = {"sn": 32, "x": 32, "w0": 16, "w1": 16, "v": 16, "pk": 16, "of2": 4, "z0": 4, "z1": 4, "z2": 4, "z3": 4}
+
+    def lanes(op, src, dst):
+        return topo.engines(src, dst)[LANES[op]]
+
+    full["po"] = 2 if TURN else 1
     for j in range(3):
-        full["g%d" % j] = full["p%d" % j] = 4
-        full["arr%d" % j] = 2 * len(topo.engines(T.cores[froms[j]], core))
+        full["g%d" % j] = 4
+        full["arr%d" % j] = sum(len(lanes(s % j, T.cores[froms[j]], core)) for s in ("sc%d", "sp%d"))
+    for c in range(len(PICKS)):
+        full["p%d" % c] = (PLAN["vec"] + PLAN["sca"]).count(" p%d" % c)
     stores = {"syn": [0, S.yd], "sca": [0, S.ye]}
 
     def move(name, out, src):
@@ -76,89 +94,116 @@ def rank_program(g, core, T, topo):
     def product(out, sq, sp, i, mq, mp):
         return g.tensor.matmul_mx(out, sq[:, 128 * i:128 * i + 128], sp[:, 128 * i:128 * i + 128], mq, mp, True, True)
 
-    def arrival_bank(j, b):
-        return (T.pa if j % 2 else T.pb)[:, 512 * b:512 * b + cap]
+    def bank(i, b, n, skip=0):
+        return (T.pb if i % 2 else T.pa)[:, 512 * b + skip:512 * b + n]
 
-    def y_bank(c, o):
+    def y_bank(c, o, skip=0):
+        lo, hi = wide(c)
+        return bank(c // 2, 2 * (c % 2) + o, hi - lo, skip)
+
+    def wide(c):
         lo, hi = CHUNKS[c]
-        i = 2 * c + o
-        return (T.pa if i < 4 else T.pb)[:, 512 * (i % 4):512 * (i % 4) + hi - lo], "fc%d%d" % (1 if i < 4 else 2, i % 4)
+        return min(lo, hi - 128), hi
+
+    def h_codes(c):
+        lo = sum(wide(i)[1] - wide(i)[0] for i in range(c))
+        hi = lo + wide(c)[1] - wide(c)[0]
+        return T.hq[:, lo:hi], T.hp[:, lo:hi]
+
+    def y_cols(c, o):
+        lo, hi = CHUNKS[c]
+        k = kh * o + (lo + TURN) % kh
+        return k, k + hi - lo
 
     def step(name, op, need):
         q = queues[name]
         kind, a = op.rstrip("0123456789"), [int(ch) for ch in op if ch.isdigit()]
         if kind == "sn":
             q.dma_start(T.sn[16 * a[0]:16 * a[0] + 16, :], T.snd[:, :]).then_inc(S.sn, 16)
-        elif op == "x":
-            q.dma_start(T.xt[:, :], T.x[:, :]).then_inc(S.x, 16)
+        elif kind == "x":
+            lo, hi = ((0, X_HEAD), (X_HEAD, 128))[a[0]]
+            q.dma_start(T.xt[lo:hi, :], T.x[lo:hi, :]).then_inc(S.x, 16)
         elif kind == "w":
-            q.dma_start(T.wt[:, 1024 * a[0]:1024 * a[0] + 1024], T.w[:, 1024 * a[0]:1024 * a[0] + 1024]).then_inc(S[op], 16)
+            lo, hi = W_PARTS[a[0]]
+            q.dma_start(T.wt[:, 512 * lo:512 * hi], T.w[:, 512 * lo:512 * hi]).then_inc(S[op], 16)
         elif op == "v":
             q.dma_start(T.vt[:, :], T.v[:, :]).then_inc(S.v, 16)
         elif op == "pk":
             q.dma_start(T.pi[:, :], T.pk[:, :]).then_inc(S.pk, 16)
-        elif op == "zero":
-            for b in range(4):
-                q.memset(T["z%d" % b][:, t_cols + cap * rank:t_cols + cap * rank + cap], 0.0).then_inc(S.zero, 1)
-        elif op == "of0":
+        elif kind == "zero":
+            c = t_cols + cap * rank + 64 * a[1]
+            q.memset(T["z%d" % a[0]][:, c:c + 64], 0.0).then_inc(S["z%d" % a[0]], 1)
+        elif op == "of2":
             need("sn")
             for p in range(0, 128, 32):
-                q.tensor_scalar(T.of0[p:p + 32, :], T.sn[0:32, :], 4.0, None, AluOpType.mult).then_inc(S.of0, 1)
-        elif op == "of1":
-            need("of0")
-            for t in (2, 1, 3):
-                q.tensor_scalar(T["of%d" % t][:, :], T.of0[:, :], float(t), None, AluOpType.add).then_inc(S.of1, 1)
+                q.tensor_scalar(T.of2[p:p + 32, :], T.sn[0:32, :], 4.0, 2.0, AluOpType.mult, AluOpType.add).then_inc(S.of2, 1)
+        elif kind == "of":
+            need("of2")
+            q.tensor_scalar(T[op][:, :], T.of2[:, :], float(a[0] - 2), None, AluOpType.add).then_inc(S[op], 1)
         elif op == "po":
             need("pk")
-            q.tensor_copy(T.po[:, :], T.pi[:, :]).then_inc(S.po, 1)
+            n = TURN // 16
+            q.tensor_copy(T.po[:, 0:32 - n], T.pi[:, n:32]).then_inc(S.po, 1)
+            if n:
+                q.tensor_copy(T.po[:, 32 - n:32], T.pi[:, 0:n]).then_inc(S.po, 1)
         elif kind == "g":
             j, t = a
-            need("of0", "of1", "x")
+            need("of%d" % t, "x")
             c = dests[j] * cap // 16
             move(name, T["st%d" % j][:, t:512:4], T.xt[:, :].indirect(T["of%d" % t][:, c:c + 8])).then_inc(S["g%d" % j], 1)
         elif kind == "q":
             need("g%d" % a[0])
             q.quantize_mx(T["sq%d" % a[0]][:, :], T["sp%d" % a[0]][:, :], T["st%d" % a[0]][:, :]).then_inc(S[op], 1)
-        elif kind == "send":
-            j = a[0]
-            dst = T.cores[dests[j]]
-            rid, pid, _ = topo.addr(dst)
-            m = topo.mask(core, dst)
-            need("q%d" % j)
-            q.remote_dma(T["lq%d" % j][:, :].bitcast(dt.uint8), T["sq%d" % j][:, :].bitcast(dt.uint8), S["arr%d" % j], S.sent, pid, rid, m)
-            q.remote_dma(T["lp%d" % j][:, :], T["sp%d" % j][:, :], S["arr%d" % j], S.sent, pid, rid, m)
-        elif op == "qx":
+        elif name == "g":
+            writes = []
+            for one in op.split("+"):
+                j = int(one[2])
+                dst = T.cores[dests[j]]
+                rid, pid, _ = topo.addr(dst)
+                need("q%d" % j)
+                if one[1] == "c":
+                    out, src = T["lq%d" % j][:, :].bitcast(dt.uint8), T["sq%d" % j][:, :].bitcast(dt.uint8)
+                else:
+                    out, src = T["lp%d" % j][:, :], T["sp%d" % j][:, :]
+                writes.append((out, src, S["arr%d" % j], pid, rid, sum(1 << e for e in lanes(one, core, dst))))
+            if len(writes) == 1:
+                out, src, sem, pid, rid, m = writes[0]
+                q.remote_dma(out, src, sem, S.sent, pid, rid, m)
+            else:
+                q.remote_dma_fused([RemoteDMATransfer(dst_ids=[DstId(rid=rid, pnc=pid)], dma_engine_mask=m, remote_sem=sem, src=src, dst=out)
+                                    for out, src, sem, pid, rid, m in writes], local_sem=S.sent)
+        elif kind == "qx":
+            lo = 256 * a[0]
             need("x")
-            q.quantize_mx(T.xq[:, :], T.xp[:, :], T.xt[:, :]).then_inc(S.qx, 1)
+            q.quantize_mx(T.xq[:, lo:lo + 256], T.xp[:, lo:lo + 256], T.xt[:, 4 * lo:4 * lo + 1024]).then_inc(S[op], 1)
         elif kind == "qw":
             b = a[0]
-            need("w%d" % (b // 2))
+            need("w%d" % (b >= W_PARTS[0][1]))
             q.quantize_mx(T.wq[:, 128 * b:128 * b + 128], T.wp[:, 128 * b:128 * b + 128], T.wt[:, 512 * b:512 * b + 512]).then_inc(S[op], 1)
         elif op == "qv":
             need("v")
             q.quantize_mx(T.vq[:, :], T.vp[:, :], T.vt[:, :]).then_inc(S.qv, 1)
         elif kind == "om":
-            b = a[0]
-            need("qx", "qw%d" % b)
-            product(T.pa[:, 512 * b:512 * b + 512], T.wq, T.wp, b, T.xq[:, :], T.xp[:, :]).then_inc(S[op], 1)
+            h, b = a
+            need("qx%d" % h, "qw%d" % b)
+            product(bank(h, b, 256), T.wq, T.wp, b, T.xq[:, 256 * h:256 * h + 256], T.xp[:, 256 * h:256 * h + 256]).then_inc(S[op], 1)
         elif kind == "oc":
-            b = a[0]
-            need("om%d" % b)
-            move(name, T["z%d" % b][:, 0:t_cols], T.pa[:, 512 * b:512 * b + 512]).then_inc(S[op], 1)
+            h, b = a
+            need("om%d%d" % (h, b))
+            move(name, T["z%d" % b][:, 256 * h:256 * h + 256], bank(h, b, 256)).then_inc(S[op], 1)
         elif kind == "fm":
             j, b = a
-            need(*([], ["oc%d" % b], ["fc0%d" % b])[j])
-            need("qw%d" % b, "arr%d" % j)
-            product(arrival_bank(j, b), T.wq, T.wp, b, T["lq%d" % j][:, :], T["lp%d" % j][:, :]).then_inc(S[op], 1)
+            need(("oc0%d", "oc1%d", "fc0%d")[j] % b, "arr%d" % j)
+            product(bank(j, b, cap), T.wq, T.wp, b, T["lq%d" % j][:, :], T["lp%d" % j][:, :]).then_inc(S[op], 1)
         elif kind == "fc":
             j, b = a
-            need("fm%d%d" % (j, b))
+            need(*(["po"] if j == 2 else []), "fm%d%d" % (j, b))
             c = t_cols + cap * froms[j]
-            move(name, T["z%d" % b][:, c:c + cap], arrival_bank(j, b)).then_inc(S[op], 1)
+            move(name, T["z%d" % b][:, c:c + cap], bank(j, b, cap)).then_inc(S["z%d" % b if j else op], 1)
         elif kind == "p":
             c, b = a
-            lo, hi = CHUNKS[c]
-            need("zero", "po", "oc%d" % b, "fc0%d" % b, "fc1%d" % b, "fc2%d" % b)
+            lo, hi = PICKS[c]
+            need("po", "z%d" % b)
             src = T["z%d" % b][:, :].indirect(T.po[:, lo // 16:hi // 16])
             out = T.ht[:, 4 * lo + b:4 * hi:4]
             if name == "vec":
@@ -166,25 +211,22 @@ def rank_program(g, core, T, topo):
             else:
                 q.activation(out, src, RELU, scale=0.05).then_inc(S["p%d" % c], 1)
         elif kind == "qh":
-            lo, hi = CHUNKS[a[0]]
-            need("p%d" % a[0])
-            q.quantize_mx(T.hq[:, lo:hi], T.hp[:, lo:hi], T.ht[:, 4 * lo:4 * hi]).then_inc(S[op], 1)
+            lo, hi = wide(a[0])
+            need(*["p%d" % c for c in range(len(PICKS)) if PICKS[c][0] < hi and lo < PICKS[c][1] and full["p%d" % c]])
+            q.quantize_mx(*h_codes(a[0]), T.ht[:, 4 * lo:4 * hi]).then_inc(S[op], 1)
         elif kind == "ym":
             c, o = a
-            lo, hi = CHUNKS[c]
-            bank, freed = y_bank(c, o)
-            need("qv", freed, "qh%d" % c)
-            product(bank, T.vq, T.vp, o, T.hq[:, lo:hi], T.hp[:, lo:hi]).then_inc(S[op], 1)
+            need("qv", "qh%d" % c)
+            product(y_bank(c, o), T.vq, T.vp, o, *h_codes(c)).then_inc(S[op], 1)
         elif kind == "yc":
             c, o = a
-            lo, hi = CHUNKS[c]
+            lo, hi = y_cols(c, o)
             need("ym%d%d" % (c, o))
-            move(name, T.ys[:, kh * o + lo:kh * o + hi], y_bank(c, o)[0]).then_inc(S[op], 1)
+            move(name, T.ys[:, lo:hi], y_bank(c, o, CHUNKS[c][0] - wide(c)[0])).then_inc(S[op], 1)
         elif kind == "st":
-            c, o = a
-            lo, hi = CHUNKS[c]
-            need("yc%d%d" % (c, o))
-            q.dma_start(T.y[:, kh * o + lo:kh * o + hi], T.ys[:, kh * o + lo:kh * o + hi]).then_inc(stores[name][1], 16)
+            lo, hi = STORES[a[0]]
+            need(*["yc%d%d" % (c, o) for c in range(len(CHUNKS)) for o in range(2) if y_cols(c, o)[0] < hi and lo < y_cols(c, o)[1]])
+            q.dma_start(T.y[:, lo:hi], T.ys[:, lo:hi]).then_inc(stores[name][1], 16)
             stores[name][0] += 16
 
     for name in PLAN:
@@ -198,7 +240,7 @@ def rank_program(g, core, T, topo):
 
         for op in PLAN[name].split():
             step(name, op, need)
-    g.wait_ge(S.sent, sum(2 * len(topo.engines(core, T.cores[d])) for d in dests))
+    g.wait_ge(S.sent, sum(len(lanes(op, core, T.cores[dests[int(op[2])]])) for op in LANES))
     for name in stores:
         if stores[name][0]:
             queues[name].wait_ge(stores[name][1], stores[name][0])

from concourse.bass import DstId, RemoteDMATransfer
from concourse.mybir import dt, AluOpType, ActivationFunctionType

RELU = ActivationFunctionType.Relu
COPY = ActivationFunctionType.Copy

PICKS = ((0, 192), (192, 384), (384, 512), (192, 512), (0, 384))
CHUNKS = ((0, 192), (192, 384), (384, 512))
STORES = ((0, 192), (512, 704), (192, 384), (704, 896), (384, 512), (896, 1024))
TURN = 0
W_PARTS = ((0, 4),)
X_HEAD = 16

SCRATCH = {
    "sn": ("sbuf", [128, 32], "int32"),
    "pi": ("sbuf", [128, 32], "int32"),
    "po": ("sbuf", [128, 32], "uint16"),
    "xt": ("sbuf", [128, 2048], "bfloat16"),
    "wt": ("sbuf", [128, 2048], "bfloat16"),
    "vt": ("sbuf", [128, 1024], "bfloat16"),
    "xq": ("sbuf", [128, 512], "float8_e4m3fn_x4"),
    "xp": ("sbuf", [128, 512], "uint8"),
    "wq": ("sbuf", [128, 512], "float8_e4m3fn_x4"),
    "wp": ("sbuf", [128, 512], "uint8"),
    "vq": ("sbuf", [128, 256], "float8_e4m3fn_x4"),
    "vp": ("sbuf", [128, 256], "uint8"),
    "ht": ("sbuf", [128, 2048], "bfloat16"),
    "hq": ("sbuf", [128, 640], "float8_e4m3fn_x4"),
    "hp": ("sbuf", [128, 640], "uint8"),
    "ys": ("sbuf", [128, 1024], "float32"),
    "pa": ("psum", [128, 2048], "float32"),
    "pb": ("psum", [128, 2048], "float32"),
}
for _t in range(4):
    SCRATCH["of%d" % _t] = ("sbuf", [128, 32], "uint16")
    SCRATCH["z%d" % _t] = ("sbuf", [128, 1024], "float32")
for _j in range(3):
    SCRATCH["st%d" % _j] = ("sbuf", [128, 512], "bfloat16")
    SCRATCH["sq%d" % _j] = ("sbuf", [128, 128], "float8_e4m3fn_x4")
    SCRATCH["sp%d" % _j] = ("sbuf", [128, 128], "uint8")
    SCRATCH["lq%d" % _j] = ("sbuf", [128, 128], "float8_e4m3fn_x4")
    SCRATCH["lp%d" % _j] = ("sbuf", [128, 128], "uint8")

PLAN = {
    "vec": "zero00 zero01 zero10 zero11 zero20 zero21 of2 zero30 of0 of3 of1 g00 g01 zero31 q0 qx0 qw0 qx1 q1 qw1 g23 qw2 q2 qw3 po qv oc01 oc03 oc13 "
           "fc01 fc03 fc11 fc13 fc21 fc23 p41 p03 p13 qh0 p21 qh1 yc01 qh2 yc11 yc21",
    "sca": "x0 x1 g02 g03 g10 g11 g12 g13 g20 g21 g22 oc00 oc10 oc11 oc02 oc12 "
           "fc00 fc02 fc10 fc12 fc20 fc22 p40 p02 p32 p20 p23 yc00 yc10 yc20 st4",
    "ten": "om00 om10 om01 om11 om02 om12 om03 om13 fm00 fm01 fm02 fm03 fm10 fm11 fm12 fm13 fm20 fm21 fm22 fm23 "
           "ym01 ym00 ym11 ym10 ym20 ym21",
    "syn": "sn0 sn1 w0 v pk st1 st0 st3 st2 st5",
    "g": "sc0 sp0 sc1 sp1 sc2 sp2",
}
EVEN, ODD, ALL = slice(0, None, 2), slice(1, None, 2), slice(None)
LANES = {"sc0": EVEN, "sp0": ODD, "sc1": ODD, "sp1": EVEN, "sc2": EVEN, "sp2": ODD}

SEMAPHORES = ["sn", "x", "w0", "w1", "v", "pk", "of0", "of1", "of2", "of3", "po", "qx0", "qx1", "qv", "sent", "yd", "ye"]
SEMAPHORES += [s % j for j in range(3) for s in ("g%d", "q%d", "arr%d")]
SEMAPHORES += ["p%d" % c for c in range(len(PICKS))] + ["qh%d" % c for c in range(len(CHUNKS))]
SEMAPHORES += [s % b for b in range(4) for s in ("qw%d", "z%d", "fc0%d")]
SEMAPHORES += [s % (h, b) for h in range(2) for b in range(4) for s in ("om%d%d", "oc%d%d")]
SEMAPHORES += ["fm%d%d" % (j, b) for j in range(3) for b in range(4)]
SEMAPHORES += [s % (c, o) for c in range(len(CHUNKS)) for o in range(2) for s in ("ym%d%d", "yc%d%d")]


def rank_program(g, core, T, topo):
    rank = T.rank_of(core)
    if rank is None:
        return
    n_ranks = len(T.cores)
    t_cols, cap, kh = 512, 128, 512
    dests = [(rank + 1 + j) % n_ranks for j in range(n_ranks - 1)]
    froms = [(rank - 1 - j) % n_ranks for j in range(n_ranks - 1)]
    S = T.sem
    queues = {"vec": g.vector, "sca": g.scalar, "ten": g.tensor, "syn": g.sync, "g": g}
    full = {"sn": 32, "x": 32, "w0": 16, "w1": 16, "v": 16, "pk": 16, "of2": 4, "z0": 4, "z1": 4, "z2": 4, "z3": 4}

    def lanes(op, src, dst):
        return topo.engines(src, dst)[LANES[op]]

    full["po"] = 2 if TURN else 1
    for j in range(3):
        full["g%d" % j] = 4
        full["arr%d" % j] = sum(len(lanes(s % j, T.cores[froms[j]], core)) for s in ("sc%d", "sp%d"))
    for c in range(len(PICKS)):
        full["p%d" % c] = (PLAN["vec"] + PLAN["sca"]).count(" p%d" % c)
    stores = {"syn": [0, S.yd], "sca": [0, S.ye]}

    def move(name, out, src):
        if name == "vec":
            return g.vector.tensor_copy(out, src)
        return g.scalar.activation(out, src, COPY)

    def product(out, sq, sp, i, mq, mp):
        return g.tensor.matmul_mx(out, sq[:, 128 * i:128 * i + 128], sp[:, 128 * i:128 * i + 128], mq, mp, True, True)

    def bank(i, b, n, skip=0):
        return (T.pb if i % 2 else T.pa)[:, 512 * b + skip:512 * b + n]

    def y_bank(c, o, skip=0):
        lo, hi = wide(c)
        return bank(c // 2, 2 * (c % 2) + o, hi - lo, skip)

    def wide(c):
        lo, hi = CHUNKS[c]
        return min(lo, hi - 128), hi

    def h_codes(c):
        lo = sum(wide(i)[1] - wide(i)[0] for i in range(c))
        hi = lo + wide(c)[1] - wide(c)[0]
        return T.hq[:, lo:hi], T.hp[:, lo:hi]

    def y_cols(c, o):
        lo, hi = CHUNKS[c]
        k = kh * o + (lo + TURN) % kh
        return k, k + hi - lo

    def step(name, op, need):
        q = queues[name]
        kind, a = op.rstrip("0123456789"), [int(ch) for ch in op if ch.isdigit()]
        if kind == "sn":
            q.dma_start(T.sn[16 * a[0]:16 * a[0] + 16, :], T.snd[:, :]).then_inc(S.sn, 16)
        elif kind == "x":
            lo, hi = ((0, X_HEAD), (X_HEAD, 128))[a[0]]
            q.dma_start(T.xt[lo:hi, :], T.x[lo:hi, :]).then_inc(S.x, 16)
        elif kind == "w":
            lo, hi = W_PARTS[a[0]]
            q.dma_start(T.wt[:, 512 * lo:512 * hi], T.w[:, 512 * lo:512 * hi]).then_inc(S[op], 16)
        elif op == "v":
            q.dma_start(T.vt[:, :], T.v[:, :]).then_inc(S.v, 16)
        elif op == "pk":
            q.dma_start(T.pi[:, :], T.pk[:, :]).then_inc(S.pk, 16)
        elif kind == "zero":
            c = t_cols + cap * rank + 64 * a[1]
            q.memset(T["z%d" % a[0]][:, c:c + 64], 0.0).then_inc(S["z%d" % a[0]], 1)
        elif op == "of2":
            need("sn")
            for p in range(0, 128, 32):
                q.tensor_scalar(T.of2[p:p + 32, :], T.sn[0:32, :], 4.0, 2.0, AluOpType.mult, AluOpType.add).then_inc(S.of2, 1)
        elif kind == "of":
            need("of2")
            q.tensor_scalar(T[op][:, :], T.of2[:, :], float(a[0] - 2), None, AluOpType.add).then_inc(S[op], 1)
        elif op == "po":
            need("pk")
            n = TURN // 16
            q.tensor_copy(T.po[:, 0:32 - n], T.pi[:, n:32]).then_inc(S.po, 1)
            if n:
                q.tensor_copy(T.po[:, 32 - n:32], T.pi[:, 0:n]).then_inc(S.po, 1)
        elif kind == "g":
            j, t = a
            need("of%d" % t, "x")
            c = dests[j] * cap // 16
            move(name, T["st%d" % j][:, t:512:4], T.xt[:, :].indirect(T["of%d" % t][:, c:c + 8])).then_inc(S["g%d" % j], 1)
        elif kind == "q":
            need("g%d" % a[0])
            q.quantize_mx(T["sq%d" % a[0]][:, :], T["sp%d" % a[0]][:, :], T["st%d" % a[0]][:, :]).then_inc(S[op], 1)
        elif name == "g":
            writes = []
            for one in op.split("+"):
                j = int(one[2])
                dst = T.cores[dests[j]]
                rid, pid, _ = topo.addr(dst)
                need("q%d" % j)
                if one[1] == "c":
                    out, src = T["lq%d" % j][:, :].bitcast(dt.uint8), T["sq%d" % j][:, :].bitcast(dt.uint8)
                else:
                    out, src = T["lp%d" % j][:, :], T["sp%d" % j][:, :]
                writes.append((out, src, S["arr%d" % j], pid, rid, sum(1 << e for e in lanes(one, core, dst))))
            if len(writes) == 1:
                out, src, sem, pid, rid, m = writes[0]
                q.remote_dma(out, src, sem, S.sent, pid, rid, m)
            else:
                q.remote_dma_fused([RemoteDMATransfer(dst_ids=[DstId(rid=rid, pnc=pid)], dma_engine_mask=m, remote_sem=sem, src=src, dst=out)
                                    for out, src, sem, pid, rid, m in writes], local_sem=S.sent)
        elif kind == "qx":
            lo = 256 * a[0]
            need("x")
            q.quantize_mx(T.xq[:, lo:lo + 256], T.xp[:, lo:lo + 256], T.xt[:, 4 * lo:4 * lo + 1024]).then_inc(S[op], 1)
        elif kind == "qw":
            b = a[0]
            need("w%d" % (b >= W_PARTS[0][1]))
            q.quantize_mx(T.wq[:, 128 * b:128 * b + 128], T.wp[:, 128 * b:128 * b + 128], T.wt[:, 512 * b:512 * b + 512]).then_inc(S[op], 1)
        elif op == "qv":
            need("v")
            q.quantize_mx(T.vq[:, :], T.vp[:, :], T.vt[:, :]).then_inc(S.qv, 1)
        elif kind == "om":
            h, b = a
            need("qx%d" % h, "qw%d" % b)
            product(bank(h, b, 256), T.wq, T.wp, b, T.xq[:, 256 * h:256 * h + 256], T.xp[:, 256 * h:256 * h + 256]).then_inc(S[op], 1)
        elif kind == "oc":
            h, b = a
            need("om%d%d" % (h, b))
            move(name, T["z%d" % b][:, 256 * h:256 * h + 256], bank(h, b, 256)).then_inc(S[op], 1)
        elif kind == "fm":
            j, b = a
            need(("oc0%d", "oc1%d", "fc0%d")[j] % b, "arr%d" % j)
            product(bank(j, b, cap), T.wq, T.wp, b, T["lq%d" % j][:, :], T["lp%d" % j][:, :]).then_inc(S[op], 1)
        elif kind == "fc":
            j, b = a
            need(*(["po"] if j == 2 else []), "fm%d%d" % (j, b))
            c = t_cols + cap * froms[j]
            move(name, T["z%d" % b][:, c:c + cap], bank(j, b, cap)).then_inc(S["z%d" % b if j else op], 1)
        elif kind == "p":
            c, b = a
            lo, hi = PICKS[c]
            need("po", "z%d" % b)
            src = T["z%d" % b][:, :].indirect(T.po[:, lo // 16:hi // 16])
            out = T.ht[:, 4 * lo + b:4 * hi:4]
            if name == "vec":
                q.tensor_scalar(out, src, 0.0, 0.05, AluOpType.max, AluOpType.mult).then_inc(S["p%d" % c], 1)
            else:
                q.activation(out, src, RELU, scale=0.05).then_inc(S["p%d" % c], 1)
        elif kind == "qh":
            lo, hi = wide(a[0])
            need(*["p%d" % c for c in range(len(PICKS)) if PICKS[c][0] < hi and lo < PICKS[c][1] and full["p%d" % c]])
            q.quantize_mx(*h_codes(a[0]), T.ht[:, 4 * lo:4 * hi]).then_inc(S[op], 1)
        elif kind == "ym":
            c, o = a
            need("qv", "qh%d" % c)
            product(y_bank(c, o), T.vq, T.vp, o, *h_codes(c)).then_inc(S[op], 1)
        elif kind == "yc":
            c, o = a
            lo, hi = y_cols(c, o)
            need("ym%d%d" % (c, o))
            move(name, T.ys[:, lo:hi], y_bank(c, o, CHUNKS[c][0] - wide(c)[0])).then_inc(S[op], 1)
        elif kind == "st":
            lo, hi = STORES[a[0]]
            need(*["yc%d%d" % (c, o) for c in range(len(CHUNKS)) for o in range(2) if y_cols(c, o)[0] < hi and lo < y_cols(c, o)[1]])
            q.dma_start(T.y[:, lo:hi], T.ys[:, lo:hi]).then_inc(stores[name][1], 16)
            stores[name][0] += 16

    for name in PLAN:
        seen = []

        def need(*sems):
            for s in sems:
                if s not in seen:
                    seen.append(s)
                    queues[name].wait_ge(S[s], full.get(s, 1))

        for op in PLAN[name].split():
            step(name, op, need)
    g.wait_ge(S.sent, sum(len(lanes(op, core, T.cores[dests[int(op[2])]])) for op in LANES))
    for name in stores:
        if stores[name][0]:
            queues[name].wait_ge(stores[name][1], stores[name][0])
